import numpy as np
import ml_dtypes


def mxq(x, axis, fmt="e4m3"):
    dtype, down = {"e4m3": (ml_dtypes.float8_e4m3fn, 7), "e5m2": (ml_dtypes.float8_e5m2, 14)}[fmt]
    v = np.moveaxis(np.asarray(x, np.float32).astype(ml_dtypes.bfloat16).astype(np.float64), axis, -1)
    blocks = v.reshape(v.shape[:-1] + (-1, 32))
    amax = np.abs(blocks).max(-1, keepdims=True)
    byte = np.maximum(np.where(amax > 0, np.frexp(amax)[1] - 1 + 127, 0) - down, 1)
    scale = np.exp2(byte - 127.0)
    codes = (blocks / scale).astype(np.float32).astype(dtype).astype(np.float64)
    return np.moveaxis((codes * scale).reshape(v.shape), -1, axis)


WIDE = False


def mx_kscale(k):
    if not WIDE:
        return np.ones(k)
    levels = np.array([30, -30])
    if k % 512:
        return np.exp2(np.random.permutation(np.resize(levels, k // 32))).repeat(32)
    a = np.empty((k // 512, 16))
    for p in range(k // 512):
        a[p, :8] = np.random.permutation(np.resize(levels, 8))
        for g in range(8):
            far = levels[np.abs(levels - a[p, g]) >= 10]
            a[p, g + 8] = far[np.random.randint(len(far))]
    return np.exp2(a.ravel()).repeat(32)


def f64(x):
    return np.asarray(x).astype(np.float64)


def striped(idx):
    return np.tile(np.asarray(idx).reshape(-1, 16).T, (8, 1)).astype(np.uint16)


def unstriped(offs):
    return offs[:16].T.reshape(-1).astype(np.int64)


E2M1 = np.array([0.0, 0.5, 1.0, 1.5, 2.0, 3.0, 4.0, 6.0, -0.0, -0.5, -1.0, -1.5, -2.0, -3.0, -4.0, -6.0])


def pack_weight(w, fmt):
    k, n = w.shape
    w = f64(np.asarray(w, np.float32).astype(ml_dtypes.bfloat16)).reshape(k // 32, 32, n)
    amax = np.abs(w).max(1)
    if fmt in ("e4m3", "e5m2"):
        byte = np.frexp(amax)[1] - 1 + 127 - (7 if fmt == "e4m3" else 14)
    else:
        mant, ex = np.frexp(amax / 6.0)
        byte = np.where(mant > 0.5, ex, ex - 1) + 127
    byte = np.clip(np.where(amax > 0, byte, 1), 1, 254)
    scaled = (w * np.exp2(127.0 - byte)[:, None, :]).reshape(k, n).astype(np.float32)
    by_word = np.ascontiguousarray(scaled.reshape(k // 512, 128, 4, n).transpose(0, 1, 3, 2))
    if fmt in ("e4m3", "e5m2"):
        words = by_word.astype(ml_dtypes.float8_e4m3fn if fmt == "e4m3" else ml_dtypes.float8_e5m2).view(np.uint8)
    else:
        c = by_word.astype(ml_dtypes.float4_e2m1fn).view(np.uint8) & 0xF
        words = (c[..., 0::2] | (c[..., 1::2] << 4)).reshape(k // 512, 128, 2 * n)
    return np.ascontiguousarray(words), np.ascontiguousarray(byte.astype(np.uint8).reshape(k // 512, 16, n))


def unpack_weight(words, scales, fmt):
    g, _, n = scales.shape
    words = np.ascontiguousarray(words).reshape(g, 128, n, -1)
    if fmt in ("e4m3", "e5m2"):
        vals = words.view(ml_dtypes.float8_e4m3fn if fmt == "e4m3" else ml_dtypes.float8_e5m2).astype(np.float64)
    else:
        nib = np.empty((g, 128, n, 4), np.uint8)
        nib[..., 0::2] = words & 0xF
        nib[..., 1::2] = words >> 4
        vals = E2M1[nib]
    vals = vals * np.repeat(np.exp2(scales.astype(np.float64) - 127.0), 8, axis=1)[..., None]
    return vals.transpose(0, 1, 3, 2).reshape(g * 512, n)


def sigmoid(v):
    return 1.0 / (1.0 + np.exp(-v))


K, F, T, Z, J, R, N, O = 512, 512, 1024, 1024, 256, 512, 256, 128


def setup_inputs():
    n = np.random.standard_normal
    idx = np.random.permutation(T)[:J]
    idx2 = np.random.permutation(Z)[:J]
    idx3 = np.random.permutation(J)[:O]
    idx4 = np.random.permutation(J)[:O]
    idx5 = np.random.permutation(J)[:O]
    fk = mx_kscale(K)
    fr = mx_kscale(R)
    ff = mx_kscale(F)
    xtp = pack_weight(n((K, T)) / fk[:, None], "e2m1")
    wp = pack_weight(n((K, R)) * 1 / np.sqrt(K) * fk[:, None] * fr, "e5m2")
    xop = pack_weight(n((F, Z)) / ff[:, None], "e5m2")
    w0p = pack_weight(n((F, R)) * 1 / np.sqrt(F) * ff[:, None] * fr, "e4m3")
    wbp = pack_weight(n((R, N)) * 1 / np.sqrt(R) / fr[:, None], "e4m3")
    wcp = pack_weight(n((R, N)) * 1 / np.sqrt(R) / fr[:, None], "e2m1")
    wdp = pack_weight(n((R, N)) * 1 / np.sqrt(R) / fr[:, None], "e4m3")
    return {
        "xt_words": xtp[0],
        "xt_scales": xtp[1],
        "w_words": wp[0],
        "w_scales": wp[1],
        "xo_words": xop[0],
        "xo_scales": xop[1],
        "w0_words": w0p[0],
        "w0_scales": w0p[1],
        "wb_words": wbp[0],
        "wb_scales": wbp[1],
        "wc_words": wcp[0],
        "wc_scales": wcp[1],
        "wd_words": wdp[0],
        "wd_scales": wdp[1],
        "so": (np.random.uniform(0.6, 1.6, (N, 1))).astype(np.float32),
        "bo": (np.random.uniform(-1.0, 1.0, (N, 1))).astype(np.float32),
        "offs": striped(idx),
        "offs2": striped(idx2),
        "offs3": striped(idx3),
        "offs4": striped(idx4),
        "offs5": striped(idx5),
    }


def reference(xt_words, xt_scales, w_words, w_scales, xo_words, xo_scales, w0_words, w0_scales, wb_words, wb_scales, wc_words, wc_scales, wd_words, wd_scales, so, bo, offs, offs2, offs3, offs4, offs5):
    idx = unstriped(offs)
    idx2 = unstriped(offs2)
    idx3 = unstriped(offs3)
    idx4 = unstriped(offs4)
    idx5 = unstriped(offs5)
    xtu = unpack_weight(xt_words, xt_scales, "e2m1")
    wu = unpack_weight(w_words, w_scales, "e5m2")
    xou = unpack_weight(xo_words, xo_scales, "e5m2")
    w0u = unpack_weight(w0_words, w0_scales, "e4m3")
    wbu = unpack_weight(wb_words, wb_scales, "e4m3")
    wcu = unpack_weight(wc_words, wc_scales, "e2m1")
    wdu = unpack_weight(wd_words, wd_scales, "e4m3")
    xtidxg = xtu[:, idx]
    xoidx2g = xou[:, idx2]
    a = wu.T @ xtidxg + w0u.T @ xoidx2g
    hid = np.maximum(a, 0.0)
    hidq = mxq(hid, 0, "e5m2")
    p = wbu.T @ hidq
    q = wcu.T @ hidq
    m0 = wdu.T @ hidq
    y = np.maximum(p[:, idx3], q[:, idx4]) * sigmoid(m0[:, idx5] * f64(so) + f64(bo))
    return y

@@ -1,0 +1,170 @@
+from contextlib import ExitStack
+
+import concourse.mybir as mybir
+
+F32 = mybir.dt.float32
+BF16 = mybir.dt.bfloat16
+I32 = mybir.dt.int32
+U32 = mybir.dt.uint32
+U16 = mybir.dt.uint16
+U8 = mybir.dt.uint8
+E4M3 = mybir.dt.float8_e4m3fn_x4
+E5M2 = mybir.dt.float8_e5m2_x4
+E2M1 = mybir.dt.float4_e2m1fn_x4
+ACT = mybir.ActivationFunctionType
+ALU = mybir.AluOpType
+
+P = 128
+T, J, R, N, O = 1024, 256, 512, 256, 128
+ROWS = 16
+FLOPS = 2 * (2 * 512 * R * J + 3 * R * N * J)
+
+
+def tile_list_threeoutcomes_bank_kernel(tc, xt_words, xt_scales, w_words, w_scales, xo_words, xo_scales, w0_words, w0_scales,
+                                               wb_words, wb_scales, wc_words, wc_scales, wd_words, wd_scales, so, bo,
+                                               offs, offs2, offs3, offs4, offs5, out):
+    nc = tc.nc
+    with ExitStack() as ctx:
+        held = ctx.enter_context(tc.tile_pool(name="held", bufs=1))
+        psum = ctx.enter_context(tc.psum_pool(name="psum", bufs=1))
+
+        def tile(shape, dtype, name):
+            return held.tile(shape, dtype, name=name, align_bytes=64)
+
+        def load_list(src, name):
+            t = held.tile(list(src.shape), U16, name=name)
+            nc.sync.dma_start(t[:], src)
+            return t
+
+        def load_words8(src, cols, name):
+            t = tile([P, cols], U32, name)
+            nc.sync.dma_start(t[:].bitcast(I32), src[0].rearrange("p n t -> p (n t)").bitcast(I32))
+            return t
+
+        def load_words4(src, cols, name):
+            t = tile([P, cols], U16, name)
+            nc.sync.dma_start(t[:].bitcast(I32), src[0].bitcast(I32))
+            return t
+
+        def load_rows(queue, dst, src):
+            queue.dma_start(dst[0:ROWS, :].bitcast(I32), src[0].bitcast(I32))
+
+        def spread(planes):
+            for q in range(1, 4):
+                nc.scalar.dma_start(planes[32 * q : 32 * q + 4, :].bitcast(I32), planes[4 * q : 4 * q + 4, :].bitcast(I32))
+
+        xt_sc = tile([P, T], U8, "xt_sc")
+        xo_sc = tile([P, T], U8, "xo_sc")
+        w_sc = tile([P, R], U8, "w_sc")
+        w0_sc = tile([P, R], U8, "w0_sc")
+        planes1 = tile([P, J + R], U8, "planes1")
+        planes2 = tile([P, J + R + 3 * N], U8, "planes2")
+        out_sc = planes2[:, J + R :]
+        nc.vector.memset(xt_sc[:].bitcast(I32), 0)
+        nc.gpsimd.memset(w_sc[:].bitcast(I32), 0)
+        nc.vector.memset(xo_sc[:].bitcast(I32), 0)
+        nc.gpsimd.memset(w0_sc[:].bitcast(I32), 0)
+        nc.vector.memset(out_sc.bitcast(I32), 0)
+
+        l1 = load_list(offs, "l1")
+        load_rows(nc.scalar, xt_sc, xt_scales)
+        load_rows(nc.scalar, w_sc, w_scales)
+        l2 = load_list(offs2, "l2")
+        load_rows(nc.scalar, xo_sc, xo_scales)
+        load_rows(nc.scalar, w0_sc, w0_scales)
+        xt_tab = load_words4(xt_words, T, "xt_tab")
+        w_raw = load_words8(w_words, R, "w_raw")
+        xo_tab = load_words8(xo_words, T, "xo_tab")
+        w0_raw = load_words8(w0_words, R, "w0_raw")
+        for i, src in enumerate((wd_scales, wb_scales, wc_scales)):
+            load_rows(nc.gpsimd, out_sc[:, N * i : N * (i + 1)], src)
+
+        xt_g = tile([P, J], U16, "xt_g")
+        xt_gs = tile([P, J], U8, "xt_gs")
+        xo_g = tile([P, J], U32, "xo_g")
+        xo_gs = tile([P, J], U8, "xo_gs")
+        w_d = tile([P, R], U32, "w_d")
+        w0_d = tile([P, R], U32, "w0_d")
+
+        def deal(copy, dst, src):
+            copy(dst.rearrange("p (t m) -> p m t", t=4), src.rearrange("p (m t) -> p m t", t=4))
+
+        nc.vector.tensor_copy(xt_gs[:], xt_sc[:].indirect(l1[:]))
+        deal(nc.vector.tensor_copy, planes1[:, J:], w_sc[:])
+        nc.vector.tensor_copy(planes1[:, 0:J].bitcast(I32), xt_gs[:].bitcast(I32))
+        spread(planes1)
+        nc.vector.tensor_copy(xo_gs[:], xo_sc[:].indirect(l2[:]))
+        deal(nc.vector.tensor_copy, planes2[:, J : J + R], w0_sc[:])
+        nc.vector.tensor_copy(planes2[:, 0:J].bitcast(I32), xo_gs[:].bitcast(I32))
+        deal(nc.scalar.copy, w_d[:], w_raw[:])
+        spread(planes2)
+        nc.vector.tensor_copy(xt_g[:], xt_tab[:].indirect(l1[:]))
+        deal(nc.scalar.copy, w0_d[:], w0_raw[:])
+        nc.vector.tensor_copy(xo_g[:], xo_tab[:].indirect(l2[:]))
+
+        wd_w = load_words8(wd_words, N, "wd_w")
+        wc_w = load_words4(wc_words, N, "wc_w")
+        wb_w = load_words8(wb_words, N, "wb_w")
+        l5 = load_list(offs5, "l5")
+        so_t = held.tile([P, 2], F32, name="so_t")
+        bo_t = held.tile([P, 2], F32, name="bo_t")
+        with nc.allow_non_contiguous_dma(reason="one value a partition"):
+            nc.sync.dma_start(so_t[:], so.rearrange("(c p) o -> p (c o)", p=P))
+            nc.sync.dma_start(bo_t[:], bo.rearrange("(c p) o -> p (c o)", p=P))
+        l3 = load_list(offs3, "l3")
+        l4 = load_list(offs4, "l4")
+
+        acc = [psum.tile([P, 4, P], F32, name="acc%d" % h) for h in range(2)]
+
+        def first_stage(h, w_dealt, w_fmt, x_g, x_fmt, planes, opens):
+            cols = slice(P * h, P * (h + 1))
+            for t in range(4):
+                nc.tensor.matmul_mx(acc[h][:, t, :], lhsT=w_dealt[:, P * t : P * (t + 1)].bitcast(w_fmt),
+                                    lhsT_scale=planes[:, J + P * t : J + P * (t + 1)],
+                                    rhs=x_g[:, cols].bitcast(x_fmt), rhs_scale=planes[:, cols],
+                                    start=(opens and t == 0), stop=(not opens and t == 3))
+
+        for h in range(2):
+            first_stage(h, w_d, E5M2, xt_g, E2M1, planes1, True)
+        hid_w = []
+        hid_s = []
+        for h in range(2):
+            first_stage(h, w0_d, E4M3, xo_g, E5M2, planes2, False)
+            hid = tile([P, P, 4], BF16, "hid%d" % h)
+            nc.scalar.activation(hid[:], acc[h][:].rearrange("p t j -> p j t"), ACT.Relu)
+            hw = tile([P, P], U32, "hid_w%d" % h)
+            hs = tile([P, P], U8, "hid_s%d" % h)
+            nc.vector.quantize_mx(out=hw[:].bitcast(E5M2), scales=hs[:], in_=hid[:].rearrange("p j t -> p (j t)"))
+            hid_w.append(hw)
+            hid_s.append(hs)
+
+        weights = {"m": (wd_w, 0, E4M3), "p": (wb_w, 1, E4M3), "q": (wc_w, 2, E2M1)}
+        pairs = [(("m", 0), ("q", 0)), (("p", 0), ("p", 1)), (("m", 1), ("q", 1))]
+        whole = {kc: tile([P, J], F32, "whole_%s%d" % kc) for pair in pairs for kc in pair}
+        gates = []
+        for h in range(2):
+            cols = slice(P * h, P * (h + 1))
+            for b, pair in enumerate(pairs):
+                bank = psum.tile([P, 2, P], F32, name="bank%d%d" % (h, b))
+                for s, (k, c) in enumerate(pair):
+                    ww, i, fmt = weights[k]
+                    nc.tensor.matmul_mx(bank[:, s, :], lhsT=ww[:, P * c : P * (c + 1)].bitcast(fmt),
+                                        lhsT_scale=out_sc[:, N * i + P * c : N * i + P * (c + 1)],
+                                        rhs=hid_w[h][:].bitcast(E5M2), rhs_scale=hid_s[h][:], start=True, stop=True)
+                for s, (k, c) in enumerate(pair):
+                    copy = nc.vector.tensor_copy if k == "p" else nc.scalar.copy
+                    copy(whole[(k, c)][:, cols], bank[:, s, :])
+                if h == 1 and pair[0][0] == "m":
+                    c = pair[0][1]
+                    gate = tile([P, O], F32, "gate%d" % c)
+                    nc.scalar.activation(gate[:], whole[("m", c)][:].indirect(l5[:]), ACT.Sigmoid,
+                                         bias=bo_t[:, c : c + 1], scale=so_t[:, c : c + 1])
+                    gates.append(gate)
+        for c in range(2):
+            pg = tile([P, O], F32, "pg%d" % c)
+            qg = tile([P, O], F32, "qg%d" % c)
+            res = tile([P, O], F32, "res%d" % c)
+            nc.vector.tensor_tensor(pg[:], whole[("p", c)][:].indirect(l3[:]), gates[c][:], ALU.mult)
+            nc.vector.tensor_tensor(qg[:], whole[("q", c)][:].indirect(l4[:]), gates[c][:], ALU.mult)
+            nc.vector.tensor_tensor(res[:], pg[:], qg[:], ALU.max)
+            nc.sync.dma_start(out[P * c : P * (c + 1), :], res[:])

@@ -65,6 +65,9 @@ def tile_list_threeoutcomes_bank_kernel(tc, xt_words, xt_scales, w_words, w_scal
         nc.vector.memset(xo_sc[:].bitcast(I32), 0)
         nc.gpsimd.memset(w0_sc[:].bitcast(I32), 0)
         nc.vector.memset(out_sc.bitcast(I32), 0)
+        warm = tile([P, 8], F32, "warm")
+        nc.gpsimd.memset(warm[:], 0.0)
+        nc.scalar.activation(warm[:, 0:1], warm[:, 4:5], ACT.Sigmoid)
 
         l1 = load_list(offs, "l1")
         load_rows(nc.scalar, xt_sc, xt_scales)

@@ -49,9 +49,9 @@ def tile_list_threeoutcomes_bank_kernel(tc, xt_words, xt_scales, w_words, w_scal
         def load_rows(queue, dst, src):
             queue.dma_start(dst[0:ROWS, :].bitcast(I32), src[0].bitcast(I32))
 
-        def spread(planes):
+        def spread(queue, planes):
             for q in range(1, 4):
-                nc.scalar.dma_start(planes[32 * q : 32 * q + 4, :].bitcast(I32), planes[4 * q : 4 * q + 4, :].bitcast(I32))
+                queue.dma_start(planes[32 * q : 32 * q + 4, :].bitcast(I32), planes[4 * q : 4 * q + 4, :].bitcast(I32))
 
         xt_sc = tile([P, T], U8, "xt_sc")
         xo_sc = tile([P, T], U8, "xo_sc")
@@ -65,22 +65,21 @@ def tile_list_threeoutcomes_bank_kernel(tc, xt_words, xt_scales, w_words, w_scal
         nc.vector.memset(xo_sc[:].bitcast(I32), 0)
         nc.gpsimd.memset(w0_sc[:].bitcast(I32), 0)
         nc.vector.memset(out_sc.bitcast(I32), 0)
+
+        l1 = load_list(offs, "l1")
+        load_rows(nc.sync, xt_sc, xt_scales)
+        load_rows(nc.scalar, w_sc, w_scales)
+        l2 = load_list(offs2, "l2")
+        load_rows(nc.sync, xo_sc, xo_scales)
+        load_rows(nc.scalar, w0_sc, w0_scales)
         warm = tile([P, 8], F32, "warm")
         nc.gpsimd.memset(warm[:], 0.0)
         nc.scalar.activation(warm[:, 0:1], warm[:, 4:5], ACT.Sigmoid)
-
-        l1 = load_list(offs, "l1")
-        load_rows(nc.scalar, xt_sc, xt_scales)
-        load_rows(nc.scalar, w_sc, w_scales)
-        l2 = load_list(offs2, "l2")
-        load_rows(nc.scalar, xo_sc, xo_scales)
-        load_rows(nc.scalar, w0_sc, w0_scales)
-        xt_tab = load_words4(xt_words, T, "xt_tab")
         w_raw = load_words8(w_words, R, "w_raw")
-        xo_tab = load_words8(xo_words, T, "xo_tab")
-        w0_raw = load_words8(w0_words, R, "w0_raw")
+        xt_tab = load_words4(xt_words, T, "xt_tab")
         for i, src in enumerate((wd_scales, wb_scales, wc_scales)):
-            load_rows(nc.gpsimd, out_sc[:, N * i : N * (i + 1)], src)
+            load_rows(nc.sync, out_sc[:, N * i : N * (i + 1)], src)
+        xo_tab = load_words8(xo_words, T, "xo_tab")
 
         xt_g = tile([P, J], U16, "xt_g")
         xt_gs = tile([P, J], U8, "xt_gs")
@@ -89,33 +88,35 @@ def tile_list_threeoutcomes_bank_kernel(tc, xt_words, xt_scales, w_words, w_scal
         w_d = tile([P, R], U32, "w_d")
         w0_d = tile([P, R], U32, "w0_d")
 
-        def deal(copy, dst, src):
-            copy(dst.rearrange("p (t m) -> p m t", t=4), src.rearrange("p (m t) -> p m t", t=4))
+        def deal(copy, dst, src, m=slice(0, P)):
+            copy(dst.rearrange("p (t m) -> p m t", t=4)[:, m, :], src.rearrange("p (m t) -> p m t", t=4)[:, m, :])
 
         nc.vector.tensor_copy(xt_gs[:], xt_sc[:].indirect(l1[:]))
         deal(nc.vector.tensor_copy, planes1[:, J:], w_sc[:])
         nc.vector.tensor_copy(planes1[:, 0:J].bitcast(I32), xt_gs[:].bitcast(I32))
-        spread(planes1)
+        spread(nc.sync, planes1)
+        w0_raw = load_words8(w0_words, R, "w0_raw")
         nc.vector.tensor_copy(xo_gs[:], xo_sc[:].indirect(l2[:]))
         deal(nc.vector.tensor_copy, planes2[:, J : J + R], w0_sc[:])
         nc.vector.tensor_copy(planes2[:, 0:J].bitcast(I32), xo_gs[:].bitcast(I32))
+        spread(nc.sync, planes2)
         deal(nc.scalar.copy, w_d[:], w_raw[:])
-        spread(planes2)
         nc.vector.tensor_copy(xt_g[:], xt_tab[:].indirect(l1[:]))
-        deal(nc.scalar.copy, w0_d[:], w0_raw[:])
         nc.vector.tensor_copy(xo_g[:], xo_tab[:].indirect(l2[:]))
+        deal(nc.scalar.copy, w0_d[:], w0_raw[:], slice(0, 48))
+        deal(nc.vector.tensor_copy, w0_d[:].bitcast(I32), w0_raw[:].bitcast(I32), slice(48, P))
 
         wd_w = load_words8(wd_words, N, "wd_w")
-        wc_w = load_words4(wc_words, N, "wc_w")
         wb_w = load_words8(wb_words, N, "wb_w")
-        l5 = load_list(offs5, "l5")
+        wc_w = load_words4(wc_words, N, "wc_w")
         so_t = held.tile([P, 2], F32, name="so_t")
         bo_t = held.tile([P, 2], F32, name="bo_t")
+        l3 = load_list(offs3, "l3")
+        l4 = load_list(offs4, "l4")
+        l5 = load_list(offs5, "l5")
         with nc.allow_non_contiguous_dma(reason="one value a partition"):
             nc.sync.dma_start(so_t[:], so.rearrange("(c p) o -> p (c o)", p=P))
             nc.sync.dma_start(bo_t[:], bo.rearrange("(c p) o -> p (c o)", p=P))
-        l3 = load_list(offs3, "l3")
-        l4 = load_list(offs4, "l4")
 
         acc = [psum.tile([P, 4, P], F32, name="acc%d" % h) for h in range(2)]
 
@@ -134,40 +135,60 @@ def tile_list_threeoutcomes_bank_kernel(tc, xt_words, xt_scales, w_words, w_scal
         for h in range(2):
             first_stage(h, w0_d, E4M3, xo_g, E5M2, planes2, False)
             hid = tile([P, P, 4], BF16, "hid%d" % h)
-            nc.scalar.activation(hid[:], acc[h][:].rearrange("p t j -> p j t"), ACT.Relu)
+            if h == 0:
+                nc.vector.tensor_scalar_max(hid[:], acc[h][:].rearrange("p t j -> p j t"), 0.0)
+            else:
+                nc.scalar.activation(hid[:], acc[h][:].rearrange("p t j -> p j t"), ACT.Relu)
             hw = tile([P, P], U32, "hid_w%d" % h)
             hs = tile([P, P], U8, "hid_s%d" % h)
             nc.vector.quantize_mx(out=hw[:].bitcast(E5M2), scales=hs[:], in_=hid[:].rearrange("p j t -> p (j t)"))
             hid_w.append(hw)
             hid_s.append(hs)
 
-        weights = {"m": (wd_w, 0, E4M3), "p": (wb_w, 1, E4M3), "q": (wc_w, 2, E2M1)}
-        pairs = [(("m", 0), ("q", 0)), (("p", 0), ("p", 1)), (("m", 1), ("q", 1))]
-        whole = {kc: tile([P, J], F32, "whole_%s%d" % kc) for pair in pairs for kc in pair}
-        gates = []
-        for h in range(2):
-            cols = slice(P * h, P * (h + 1))
-            for b, pair in enumerate(pairs):
-                bank = psum.tile([P, 2, P], F32, name="bank%d%d" % (h, b))
-                for s, (k, c) in enumerate(pair):
-                    ww, i, fmt = weights[k]
-                    nc.tensor.matmul_mx(bank[:, s, :], lhsT=ww[:, P * c : P * (c + 1)].bitcast(fmt),
-                                        lhsT_scale=out_sc[:, N * i + P * c : N * i + P * (c + 1)],
-                                        rhs=hid_w[h][:].bitcast(E5M2), rhs_scale=hid_s[h][:], start=True, stop=True)
-                for s, (k, c) in enumerate(pair):
-                    copy = nc.vector.tensor_copy if k == "p" else nc.scalar.copy
-                    copy(whole[(k, c)][:, cols], bank[:, s, :])
-                if h == 1 and pair[0][0] == "m":
-                    c = pair[0][1]
-                    gate = tile([P, O], F32, "gate%d" % c)
-                    nc.scalar.activation(gate[:], whole[("m", c)][:].indirect(l5[:]), ACT.Sigmoid,
-                                         bias=bo_t[:, c : c + 1], scale=so_t[:, c : c + 1])
-                    gates.append(gate)
-        for c in range(2):
-            pg = tile([P, O], F32, "pg%d" % c)
-            qg = tile([P, O], F32, "qg%d" % c)
-            res = tile([P, O], F32, "res%d" % c)
-            nc.vector.tensor_tensor(pg[:], whole[("p", c)][:].indirect(l3[:]), gates[c][:], ALU.mult)
-            nc.vector.tensor_tensor(qg[:], whole[("q", c)][:].indirect(l4[:]), gates[c][:], ALU.mult)
-            nc.vector.tensor_tensor(res[:], pg[:], qg[:], ALU.max)
-            nc.sync.dma_start(out[P * c : P * (c + 1), :], res[:])
+        def second_stage(dst, ww, i, fmt, c, h):
+            nc.tensor.matmul_mx(dst, lhsT=ww[:, P * c : P * (c + 1)].bitcast(fmt),
+                                lhsT_scale=out_sc[:, N * i + P * c : N * i + P * (c + 1)],
+                                rhs=hid_w[h][:].bitcast(E5M2), rhs_scale=hid_s[h][:], start=True, stop=True)
+
+        m_all = [tile([P, J], F32, "m_all%d" % c) for c in range(2)]
+        pq_all = [tile([P, 2, J], F32, "pq_all%d" % c) for c in range(2)]
+
+        def third_outcome(h):
+            bank = psum.tile([P, 2, P], F32, name="m_bank%d" % h)
+            for c in range(2):
+                second_stage(bank[:, c, :], wd_w, 0, E4M3, c, h)
+            for c in range(2):
+                nc.scalar.copy(m_all[c][:, P * h : P * (h + 1)], bank[:, c, :])
+
+        def first_outcomes(h, c, copy):
+            bank = psum.tile([P, 2, P], F32, name="pq_bank%d%d" % (h, c))
+            second_stage(bank[:, 0, :], wb_w, 1, E4M3, c, h)
+            second_stage(bank[:, 1, :], wc_w, 2, E2M1, c, h)
+            copy(pq_all[c][:, :, P * h : P * (h + 1)], bank[:])
+
+        third_outcome(0)
+        first_outcomes(0, 0, nc.vector.tensor_copy)
+        first_outcomes(0, 1, nc.scalar.copy)
+        third_outcome(1)
+        first_outcomes(1, 1, nc.vector.tensor_copy)
+        first_outcomes(1, 0, nc.scalar.copy)
+        gate = [tile([P, O], F32, "gate%d" % c) for c in range(2)]
+        pg = [tile([P, O], F32, "pg%d" % c) for c in range(2)]
+        qg = [tile([P, O], F32, "qg%d" % c) for c in range(2)]
+        top = [tile([P, O], F32, "top%d" % c) for c in range(2)]
+        res = [tile([P, O], F32, "res%d" % c) for c in range(2)]
+
+        def look(c):
+            nc.scalar.activation(gate[c][:], m_all[c][:].indirect(l5[:]), ACT.Sigmoid, bias=bo_t[:, c : c + 1], scale=so_t[:, c : c + 1])
+
+        nc.scalar.activation(qg[1][:], pq_all[1][:, 1, :].indirect(l4[:]), ACT.Copy)
+        look(1)
+        look(0)
+        nc.vector.tensor_copy(pg[1][:], pq_all[1][:, 0, :].indirect(l3[:]))
+        nc.vector.tensor_copy(pg[0][:], pq_all[0][:, 0, :].indirect(l3[:]))
+        nc.vector.tensor_copy(qg[0][:], pq_all[0][:, 1, :].indirect(l4[:]))
+        for c in (1, 0):
+            nc.vector.tensor_tensor(top[c][:], pg[c][:], qg[c][:], ALU.max)
+        for c in (1, 0):
+            nc.vector.tensor_tensor(res[c][:], top[c][:], gate[c][:], ALU.mult)
+            nc.sync.dma_start(out[P * c : P * (c + 1), :], res[c][:])

@@ -17,6 +17,7 @@ ALU = mybir.AluOpType
 P = 128
 T, J, R, N, O = 1024, 256, 512, 256, 128
 ROWS = 16
+TOP = P - ROWS
 FLOPS = 2 * (2 * 512 * R * J + 3 * R * N * J)
 
 
@@ -46,12 +47,14 @@ def tile_list_threeoutcomes_bank_kernel(tc, xt_words, xt_scales, w_words, w_scal
             nc.sync.dma_start(t[:].bitcast(I32), src[0].bitcast(I32))
             return t
 
-        def load_rows(queue, dst, src):
-            queue.dma_start(dst[0:ROWS, :].bitcast(I32), src[0].bitcast(I32))
+        def load_rows(queue, dst, src, first=0):
+            queue.dma_start(dst[first : first + ROWS, :].bitcast(I32), src[0].bitcast(I32))
 
-        def spread(queue, planes):
-            for q in range(1, 4):
-                queue.dma_start(planes[32 * q : 32 * q + 4, :].bitcast(I32), planes[4 * q : 4 * q + 4, :].bitcast(I32))
+        def spread(queue, planes, first=0):
+            for q in range(4):
+                row = first + 4 * q
+                if row != 32 * q:
+                    queue.dma_start(planes[32 * q : 32 * q + 4, :].bitcast(I32), planes[row : row + 4, :].bitcast(I32))
 
         xt_sc = tile([P, T], U8, "xt_sc")
         xo_sc = tile([P, T], U8, "xo_sc")
@@ -60,25 +63,28 @@ def tile_list_threeoutcomes_bank_kernel(tc, xt_words, xt_scales, w_words, w_scal
         planes1 = tile([P, J + R], U8, "planes1")
         planes2 = tile([P, J + R + 3 * N], U8, "planes2")
         out_sc = planes2[:, J + R :]
-        nc.vector.memset(xt_sc[:].bitcast(I32), 0)
-        nc.gpsimd.memset(w_sc[:].bitcast(I32), 0)
+        warm = tile([P, 8], F32, "warm")
+        nc.gpsimd.memset(out_sc[:, 2 * N :].bitcast(I32), 0)
         nc.vector.memset(xo_sc[:].bitcast(I32), 0)
-        nc.gpsimd.memset(w0_sc[:].bitcast(I32), 0)
-        nc.vector.memset(out_sc.bitcast(I32), 0)
+        nc.vector.memset(w0_sc[:].bitcast(I32), 0)
+        nc.vector.memset(warm[:], 0.0)
+        nc.vector.memset(xt_sc[0:TOP, :].bitcast(I32), 0)
+        nc.vector.memset(w_sc[0:TOP, :].bitcast(I32), 0)
+        nc.vector.memset(out_sc[:, 0 : 2 * N].bitcast(I32), 0)
 
         l1 = load_list(offs, "l1")
-        load_rows(nc.sync, xt_sc, xt_scales)
-        load_rows(nc.scalar, w_sc, w_scales)
+        load_rows(nc.scalar, xt_sc, xt_scales, TOP)
+        load_rows(nc.scalar, w_sc, w_scales, TOP)
         l2 = load_list(offs2, "l2")
         load_rows(nc.sync, xo_sc, xo_scales)
-        load_rows(nc.scalar, w0_sc, w0_scales)
-        warm = tile([P, 8], F32, "warm")
-        nc.gpsimd.memset(warm[:], 0.0)
+        load_rows(nc.sync, w0_sc, w0_scales)
+        load_rows(nc.gpsimd, out_sc[:, 2 * N :], wc_scales)
         nc.scalar.activation(warm[:, 0:1], warm[:, 4:5], ACT.Sigmoid)
         w_raw = load_words8(w_words, R, "w_raw")
         xt_tab = load_words4(xt_words, T, "xt_tab")
-        for i, src in enumerate((wd_scales, wb_scales, wc_scales)):
-            load_rows(nc.sync, out_sc[:, N * i : N * (i + 1)], src)
+        load_rows(nc.sync, out_sc[:, 0:N], wd_scales)
+        load_rows(nc.sync, out_sc[:, N : 2 * N], wb_scales)
+        w0_raw = load_words8(w0_words, R, "w0_raw")
         xo_tab = load_words8(xo_words, T, "xo_tab")
 
         xt_g = tile([P, J], U16, "xt_g")
@@ -88,23 +94,21 @@ def tile_list_threeoutcomes_bank_kernel(tc, xt_words, xt_scales, w_words, w_scal
         w_d = tile([P, R], U32, "w_d")
         w0_d = tile([P, R], U32, "w0_d")
 
-        def deal(copy, dst, src, m=slice(0, P)):
-            copy(dst.rearrange("p (t m) -> p m t", t=4)[:, m, :], src.rearrange("p (m t) -> p m t", t=4)[:, m, :])
+        def deal(copy, dst, src):
+            copy(dst.rearrange("p (t m) -> p m t", t=4), src.rearrange("p (m t) -> p m t", t=4))
 
         nc.vector.tensor_copy(xt_gs[:], xt_sc[:].indirect(l1[:]))
         deal(nc.vector.tensor_copy, planes1[:, J:], w_sc[:])
         nc.vector.tensor_copy(planes1[:, 0:J].bitcast(I32), xt_gs[:].bitcast(I32))
-        spread(nc.sync, planes1)
-        w0_raw = load_words8(w0_words, R, "w0_raw")
+        spread(nc.sync, planes1, TOP)
         nc.vector.tensor_copy(xo_gs[:], xo_sc[:].indirect(l2[:]))
         deal(nc.vector.tensor_copy, planes2[:, J : J + R], w0_sc[:])
         nc.vector.tensor_copy(planes2[:, 0:J].bitcast(I32), xo_gs[:].bitcast(I32))
         spread(nc.sync, planes2)
         deal(nc.scalar.copy, w_d[:], w_raw[:])
         nc.vector.tensor_copy(xt_g[:], xt_tab[:].indirect(l1[:]))
+        deal(nc.scalar.copy, w0_d[:], w0_raw[:])
         nc.vector.tensor_copy(xo_g[:], xo_tab[:].indirect(l2[:]))
-        deal(nc.scalar.copy, w0_d[:], w0_raw[:], slice(0, 48))
-        deal(nc.vector.tensor_copy, w0_d[:].bitcast(I32), w0_raw[:].bitcast(I32), slice(48, P))
 
         wd_w = load_words8(wd_words, N, "wd_w")
         wb_w = load_words8(wb_words, N, "wb_w")

from contextlib import ExitStack

import concourse.mybir as mybir

F32 = mybir.dt.float32
BF16 = mybir.dt.bfloat16
I32 = mybir.dt.int32
U32 = mybir.dt.uint32
U16 = mybir.dt.uint16
U8 = mybir.dt.uint8
E4M3 = mybir.dt.float8_e4m3fn_x4
E5M2 = mybir.dt.float8_e5m2_x4
E2M1 = mybir.dt.float4_e2m1fn_x4
ACT = mybir.ActivationFunctionType
ALU = mybir.AluOpType

P = 128
T, J, R, N, O = 1024, 256, 512, 256, 128
ROWS = 16
TOP = P - ROWS
FLOPS = 2 * (2 * 512 * R * J + 3 * R * N * J)


def tile_list_threeoutcomes_bank_kernel(tc, xt_words, xt_scales, w_words, w_scales, xo_words, xo_scales, w0_words, w0_scales,
                                               wb_words, wb_scales, wc_words, wc_scales, wd_words, wd_scales, so, bo,
                                               offs, offs2, offs3, offs4, offs5, out):
    nc = tc.nc
    with ExitStack() as ctx:
        held = ctx.enter_context(tc.tile_pool(name="held", bufs=1))
        psum = ctx.enter_context(tc.psum_pool(name="psum", bufs=1))

        def tile(shape, dtype, name):
            return held.tile(shape, dtype, name=name, align_bytes=64)

        def load_list(src, name):
            t = held.tile(list(src.shape), U16, name=name)
            nc.sync.dma_start(t[:], src)
            return t

        def load_words8(src, cols, name):
            t = tile([P, cols], U32, name)
            nc.sync.dma_start(t[:].bitcast(I32), src[0].rearrange("p n t -> p (n t)").bitcast(I32))
            return t

        def load_words4(src, cols, name):
            t = tile([P, cols], U16, name)
            nc.sync.dma_start(t[:].bitcast(I32), src[0].bitcast(I32))
            return t

        def load_rows(queue, dst, src, first=0):
            queue.dma_start(dst[first : first + ROWS, :].bitcast(I32), src[0].bitcast(I32))

        def spread(queue, planes, first=0):
            for q in range(4):
                row = first + 4 * q
                if row != 32 * q:
                    queue.dma_start(planes[32 * q : 32 * q + 4, :].bitcast(I32), planes[row : row + 4, :].bitcast(I32))

        xt_sc = tile([P, T], U8, "xt_sc")
        xo_sc = tile([P, T], U8, "xo_sc")
        w_sc = tile([P, R], U8, "w_sc")
        w0_sc = tile([P, R], U8, "w0_sc")
        planes1 = tile([P, J + R], U8, "planes1")
        planes2 = tile([P, J + R + 3 * N], U8, "planes2")
        out_sc = planes2[:, J + R :]
        warm = tile([P, 8], F32, "warm")
        nc.gpsimd.memset(out_sc[:, 2 * N :].bitcast(I32), 0)
        nc.vector.memset(xo_sc[:].bitcast(I32), 0)
        nc.vector.memset(w0_sc[:].bitcast(I32), 0)
        nc.vector.memset(warm[:], 0.0)
        nc.vector.memset(xt_sc[0:TOP, :].bitcast(I32), 0)
        nc.vector.memset(w_sc[0:TOP, :].bitcast(I32), 0)
        nc.vector.memset(out_sc[:, 0 : 2 * N].bitcast(I32), 0)

        l1 = load_list(offs, "l1")
        load_rows(nc.scalar, xt_sc, xt_scales, TOP)
        load_rows(nc.scalar, w_sc, w_scales, TOP)
        l2 = load_list(offs2, "l2")
        load_rows(nc.sync, xo_sc, xo_scales)
        load_rows(nc.sync, w0_sc, w0_scales)
        load_rows(nc.gpsimd, out_sc[:, 2 * N :], wc_scales)
        nc.scalar.activation(warm[:, 0:1], warm[:, 4:5], ACT.Sigmoid)
        w_raw = load_words8(w_words, R, "w_raw")
        xt_tab = load_words4(xt_words, T, "xt_tab")
        load_rows(nc.sync, out_sc[:, 0:N], wd_scales)
        load_rows(nc.sync, out_sc[:, N : 2 * N], wb_scales)
        w0_raw = load_words8(w0_words, R, "w0_raw")
        xo_tab = load_words8(xo_words, T, "xo_tab")

        xt_g = tile([P, J], U16, "xt_g")
        xt_gs = tile([P, J], U8, "xt_gs")
        xo_g = tile([P, J], U32, "xo_g")
        xo_gs = tile([P, J], U8, "xo_gs")
        w_d = tile([P, R], U32, "w_d")
        w0_d = tile([P, R], U32, "w0_d")

        def deal(copy, dst, src):
            copy(dst.rearrange("p (t m) -> p m t", t=4), src.rearrange("p (m t) -> p m t", t=4))

        nc.vector.tensor_copy(xt_gs[:], xt_sc[:].indirect(l1[:]))
        deal(nc.vector.tensor_copy, planes1[:, J:], w_sc[:])
        nc.vector.tensor_copy(planes1[:, 0:J].bitcast(I32), xt_gs[:].bitcast(I32))
        spread(nc.sync, planes1, TOP)
        nc.vector.tensor_copy(xo_gs[:], xo_sc[:].indirect(l2[:]))
        deal(nc.vector.tensor_copy, planes2[:, J : J + R], w0_sc[:])
        nc.vector.tensor_copy(planes2[:, 0:J].bitcast(I32), xo_gs[:].bitcast(I32))
        spread(nc.sync, planes2)
        deal(nc.scalar.copy, w_d[:], w_raw[:])
        nc.vector.tensor_copy(xt_g[:], xt_tab[:].indirect(l1[:]))
        deal(nc.scalar.copy, w0_d[:], w0_raw[:])
        nc.vector.tensor_copy(xo_g[:], xo_tab[:].indirect(l2[:]))

        wd_w = load_words8(wd_words, N, "wd_w")
        wb_w = load_words8(wb_words, N, "wb_w")
        wc_w = load_words4(wc_words, N, "wc_w")
        so_t = held.tile([P, 2], F32, name="so_t")
        bo_t = held.tile([P, 2], F32, name="bo_t")
        l3 = load_list(offs3, "l3")
        l4 = load_list(offs4, "l4")
        l5 = load_list(offs5, "l5")
        with nc.allow_non_contiguous_dma(reason="one value a partition"):
            nc.sync.dma_start(so_t[:], so.rearrange("(c p) o -> p (c o)", p=P))
            nc.sync.dma_start(bo_t[:], bo.rearrange("(c p) o -> p (c o)", p=P))

        acc = [psum.tile([P, 4, P], F32, name="acc%d" % h) for h in range(2)]

        def first_stage(h, w_dealt, w_fmt, x_g, x_fmt, planes, opens):
            cols = slice(P * h, P * (h + 1))
            for t in range(4):
                nc.tensor.matmul_mx(acc[h][:, t, :], lhsT=w_dealt[:, P * t : P * (t + 1)].bitcast(w_fmt),
                                    lhsT_scale=planes[:, J + P * t : J + P * (t + 1)],
                                    rhs=x_g[:, cols].bitcast(x_fmt), rhs_scale=planes[:, cols],
                                    start=(opens and t == 0), stop=(not opens and t == 3))

        for h in range(2):
            first_stage(h, w_d, E5M2, xt_g, E2M1, planes1, True)
        hid_w = []
        hid_s = []
        for h in range(2):
            first_stage(h, w0_d, E4M3, xo_g, E5M2, planes2, False)
            hid = tile([P, P, 4], BF16, "hid%d" % h)
            if h == 0:
                nc.vector.tensor_scalar_max(hid[:], acc[h][:].rearrange("p t j -> p j t"), 0.0)
            else:
                nc.scalar.activation(hid[:], acc[h][:].rearrange("p t j -> p j t"), ACT.Relu)
            hw = tile([P, P], U32, "hid_w%d" % h)
            hs = tile([P, P], U8, "hid_s%d" % h)
            nc.vector.quantize_mx(out=hw[:].bitcast(E5M2), scales=hs[:], in_=hid[:].rearrange("p j t -> p (j t)"))
            hid_w.append(hw)
            hid_s.append(hs)

        def second_stage(dst, ww, i, fmt, c, h):
            nc.tensor.matmul_mx(dst, lhsT=ww[:, P * c : P * (c + 1)].bitcast(fmt),
                                lhsT_scale=out_sc[:, N * i + P * c : N * i + P * (c + 1)],
                                rhs=hid_w[h][:].bitcast(E5M2), rhs_scale=hid_s[h][:], start=True, stop=True)

        m_all = [tile([P, J], F32, "m_all%d" % c) for c in range(2)]
        pq_all = [tile([P, 2, J], F32, "pq_all%d" % c) for c in range(2)]

        def third_outcome(h):
            bank = psum.tile([P, 2, P], F32, name="m_bank%d" % h)
            for c in range(2):
                second_stage(bank[:, c, :], wd_w, 0, E4M3, c, h)
            for c in range(2):
                nc.scalar.copy(m_all[c][:, P * h : P * (h + 1)], bank[:, c, :])

        def first_outcomes(h, c, copy):
            bank = psum.tile([P, 2, P], F32, name="pq_bank%d%d" % (h, c))
            second_stage(bank[:, 0, :], wb_w, 1, E4M3, c, h)
            second_stage(bank[:, 1, :], wc_w, 2, E2M1, c, h)
            copy(pq_all[c][:, :, P * h : P * (h + 1)], bank[:])

        third_outcome(0)
        first_outcomes(0, 0, nc.vector.tensor_copy)
        first_outcomes(0, 1, nc.scalar.copy)
        third_outcome(1)
        first_outcomes(1, 1, nc.vector.tensor_copy)
        first_outcomes(1, 0, nc.scalar.copy)
        gate = [tile([P, O], F32, "gate%d" % c) for c in range(2)]
        pg = [tile([P, O], F32, "pg%d" % c) for c in range(2)]
        qg = [tile([P, O], F32, "qg%d" % c) for c in range(2)]
        top = [tile([P, O], F32, "top%d" % c) for c in range(2)]
        res = [tile([P, O], F32, "res%d" % c) for c in range(2)]

        def look(c):
            nc.scalar.activation(gate[c][:], m_all[c][:].indirect(l5[:]), ACT.Sigmoid, bias=bo_t[:, c : c + 1], scale=so_t[:, c : c + 1])

        nc.scalar.activation(qg[1][:], pq_all[1][:, 1, :].indirect(l4[:]), ACT.Copy)
        look(1)
        look(0)
        nc.vector.tensor_copy(pg[1][:], pq_all[1][:, 0, :].indirect(l3[:]))
        nc.vector.tensor_copy(pg[0][:], pq_all[0][:, 0, :].indirect(l3[:]))
        nc.vector.tensor_copy(qg[0][:], pq_all[0][:, 1, :].indirect(l4[:]))
        for c in (1, 0):
            nc.vector.tensor_tensor(top[c][:], pg[c][:], qg[c][:], ALU.max)
        for c in (1, 0):
            nc.vector.tensor_tensor(res[c][:], top[c][:], gate[c][:], ALU.mult)
            nc.sync.dma_start(out[P * c : P * (c + 1), :], res[c][:])
